import numpy as np
import ml_dtypes


def mxq(x, axis, fmt="e4m3"):
    dtype, down = {"e4m3": (ml_dtypes.float8_e4m3fn, 7), "e5m2": (ml_dtypes.float8_e5m2, 14)}[fmt]
    v = np.moveaxis(np.asarray(x, np.float32).astype(ml_dtypes.bfloat16).astype(np.float64), axis, -1)
    blocks = v.reshape(v.shape[:-1] + (-1, 32))
    amax = np.abs(blocks).max(-1, keepdims=True)
    byte = np.maximum(np.where(amax > 0, np.frexp(amax)[1] - 1 + 127, 0) - down, 1)
    scale = np.exp2(byte - 127.0)
    codes = (blocks / scale).astype(np.float32).astype(dtype).astype(np.float64)
    return np.moveaxis((codes * scale).reshape(v.shape), -1, axis)


WIDE = False


def mx_kscale(k):
    if not WIDE:
        return np.ones(k)
    levels = np.array([10, -10, 5, -5, 0])
    if k % 512:
        return np.exp2(np.random.permutation(np.resize(levels, k // 32))).repeat(32)
    a = np.empty((k // 512, 16))
    for p in range(k // 512):
        a[p, :8] = np.random.permutation(np.resize(levels, 8))
        for g in range(8):
            far = levels[np.abs(levels - a[p, g]) >= 10]
            a[p, g + 8] = far[np.random.randint(len(far))]
    return np.exp2(a.ravel()).repeat(32)


def f64(x):
    return np.asarray(x).astype(np.float64)


def striped(idx):
    return np.tile(idx.reshape(-1, 16).T, (8, 1)).astype(np.uint16)


def unstriped(offs):
    return offs[:16].T.reshape(-1).astype(np.int64)


def striped8(idx):
    return np.concatenate([x.reshape(-1, 16).T for x in idx]).astype(np.uint16)


def runs(offs, k):
    lists = np.stack([offs[16 * r : 16 * r + 16].T.reshape(-1) for r in range(8)]).astype(np.int64)
    return lists[np.arange(k) % 512 // 64]


def pack_weight(w):
    k, n = w.shape
    w = f64(np.asarray(w, np.float32).astype(ml_dtypes.bfloat16)).reshape(k // 32, 32, n)
    amax = np.abs(w).max(1)
    byte = np.clip(np.where(amax > 0, np.frexp(amax)[1] - 1 + 127 - 7, 1), 1, 254)
    scaled = (w * np.exp2(127.0 - byte)[:, None, :]).reshape(k, n).astype(np.float32)
    words = np.ascontiguousarray(scaled.reshape(k // 512, 128, 4, n).transpose(0, 1, 3, 2)).astype(ml_dtypes.float8_e4m3fn).view(np.uint8)
    return words, np.ascontiguousarray(byte.astype(np.uint8).reshape(k // 512, 16, n))


def unpack_weight(words, scales):
    g, p, n, _ = words.shape
    vals = np.ascontiguousarray(words).view(ml_dtypes.float8_e4m3fn).astype(np.float64) * np.repeat(np.exp2(scales.astype(np.float64) - 127.0), 8, axis=1)[..., None]
    return vals.transpose(0, 1, 3, 2).reshape(g * 512, n)


K, T, S, V, H = 512, 2048, 512, 512, 512


def setup_inputs():
    n = np.random.standard_normal
    s = mx_kscale(K)[:, None]
    u = mx_kscale(S)
    packed_xT = pack_weight(n((K, T)) * s)
    return {
        "x_words": packed_xT[0],
        "x_scales": packed_xT[1],
        "w1": (n((K, H)) / np.sqrt(K) / s).astype(np.float32),
        "w2": (n((K, H)) / np.sqrt(K) / s).astype(np.float32),
        "w3": (n((K, H)) / np.sqrt(K) / s).astype(np.float32),
        "ga": (np.random.uniform(0.5, 1.5, (H, 1)) * u[:, None]).astype(np.float32),
        "gb": (np.random.uniform(0.5, 1.5, (H, 1)) / u[:, None]).astype(np.float32),
        "offs": striped(np.random.permutation(T)[:S]),
        "two": striped(np.random.permutation(T)[:S]),
        "n1": striped8(np.stack([np.random.permutation(S) for _ in range(8)])),
        "n2": striped8(np.stack([np.random.permutation(S) for _ in range(8)])),
        "n3": striped8(np.stack([np.random.permutation(S) for _ in range(8)])),
        "n4": striped8(np.stack([np.random.permutation(S) for _ in range(8)])),
        "three": striped(np.random.permutation(T)[:V]),
        "n5": striped8(np.stack([np.random.permutation(V) for _ in range(8)])),
        "n6": striped8(np.stack([np.random.permutation(V) for _ in range(8)])),
        "n7": striped8(np.stack([np.random.permutation(V) for _ in range(8)])),
        "n8": striped8(np.stack([np.random.permutation(V) for _ in range(8)])),
        "n9": striped8(np.stack([np.random.permutation(V) for _ in range(8)])),
    }


def reference(x_words, x_scales, w1, w2, w3, ga, gb, offs, two, n1, n2, n3, n4, three, n5, n6, n7, n8, n9):
    xq = unpack_weight(x_words, x_scales)[:, unstriped(offs)]
    y = mxq(f64(w1), 0, "e4m3").T @ xq
    x_two = unpack_weight(x_words, x_scales)[:, unstriped(two)]
    d = mxq(f64(w2), 0, "e4m3").T @ x_two
    z = f64(ga) * (np.maximum(y[np.arange(H)[:, None], runs(n1, H)] + d[np.arange(H)[:, None], runs(n3, H)], y[np.arange(H)[:, None], runs(n2, H)] + d[np.arange(H)[:, None], runs(n4, H)]))
    x_three = unpack_weight(x_words, x_scales)[:, unstriped(three)]
    b = mxq(f64(w3), 0, "e4m3").T @ x_three
    z2 = f64(gb) * (b * (b[np.arange(H)[:, None], runs(n5, H)] - (b[np.arange(H)[:, None], runs(n6, H)])))
    s = 0.0625 * ((mxq(z, 0, "e4m3").T @ mxq(z2, 0, "e4m3")))
    st = s - (s[np.arange(S)[:, None], runs(n7, S)])
    su = np.maximum(st, st[np.arange(S)[:, None], runs(n8, S)])
    return su + 0.5 * (su[np.arange(S)[:, None], runs(n9, S)])

@@ -1,0 +1,254 @@
+from contextlib import ExitStack
+
+import concourse.mybir as mybir
+
+K, T, S, V, H = 512, 2048, 512, 512, 512
+FLOPS = 2 * K * H * (S + S + V) + 2 * H * S * V
+
+F32 = mybir.dt.float32
+BF16 = mybir.dt.bfloat16
+I32 = mybir.dt.int32
+U32 = mybir.dt.uint32
+U16 = mybir.dt.uint16
+U8 = mybir.dt.uint8
+FP8X4 = mybir.dt.float8_e4m3fn_x4
+ALU = mybir.AluOpType
+COPY = mybir.ActivationFunctionType.Copy
+
+P = 128
+PACK = 4
+HALF = 256
+STRIPE = 16
+
+
+def tile_picked_twkpathbwindthree_none_p_kernel(
+    tc, x_words, x_scales, w1, w2, w3, ga, gb, offs, two, n1, n2, n3, n4, three, n5, n6, n7, n8, n9, out
+):
+    nc = tc.nc
+    with ExitStack() as ctx:
+        lists = ctx.enter_context(tc.tile_pool(name="lists", bufs=1))
+        keep = ctx.enter_context(tc.tile_pool(name="keep", bufs=1))
+        ring = ctx.enter_context(tc.tile_pool(name="ring", bufs=3))
+        psum = ctx.enter_context(tc.psum_pool(name="psum", bufs=8))
+
+        def load_list(name, src):
+            tile = lists.tile([P, S // STRIPE], U16, name=name)
+            nc.sync.dma_start(tile[:], src)
+            return tile
+
+        def load_weight(name, src):
+            raw = keep.tile([P, PACK, H], F32, name=name)
+            nc.sync.dma_start(out=raw[:], in_=src.rearrange("(p j) c -> p j c", j=PACK))
+            return raw
+
+        def half_of(offsets, h):
+            return offsets[:, h * HALF // STRIPE : (h + 1) * HALF // STRIPE]
+
+        def cols(h):
+            return slice(h * HALF, (h + 1) * HALF)
+
+        plane = keep.tile([P, T], U8, name="plane", align_bytes=64)
+        nc.vector.memset(plane[:].bitcast(I32), 0)
+        l_three = load_list("l_three", three)
+        for q in range(4):
+            nc.scalar.dma_start(out=plane[32 * q : 32 * q + 4, :].bitcast(I32), in_=x_scales[0, 4 * q : 4 * q + 4, :].bitcast(I32))
+        words = keep.tile([P, T], U32, name="words", align_bytes=64)
+        nc.sync.dma_start(out=words[:].bitcast(I32), in_=x_words[0].rearrange("p n t -> p (n t)").bitcast(I32))
+        l_offs = load_list("l_offs", offs)
+        l_two = load_list("l_two", two)
+        raw3 = load_weight("raw3", w3)
+        l5 = load_list("l5", n5)
+        l6 = load_list("l6", n6)
+        raw1 = load_weight("raw1", w1)
+        raw2 = load_weight("raw2", w2)
+        l1 = load_list("l1", n1)
+        l2 = load_list("l2", n2)
+        l3 = load_list("l3", n3)
+        l4 = load_list("l4", n4)
+        l7 = load_list("l7", n7)
+        l8 = load_list("l8", n8)
+        l9 = load_list("l9", n9)
+
+        ga_t = keep.tile([P, PACK], F32, name="ga_t")
+        gb_t = keep.tile([P, PACK], F32, name="gb_t")
+        nc.gpsimd.dma_start(out=ga_t[:], in_=ga.rearrange("(p t) o -> p (t o)", t=PACK))
+        nc.gpsimd.dma_start(out=gb_t[:], in_=gb.rearrange("(p t) o -> p (t o)", t=PACK))
+        twice = keep.tile([P, PACK], F32, name="twice")
+        sign = keep.tile([P, PACK], F32, name="sign")
+        ga_abs = keep.tile([P, PACK], F32, name="ga_abs")
+        gb_signed = keep.tile([P, PACK], F32, name="gb_signed")
+        nc.gpsimd.tensor_scalar(twice[:], ga_t[:], 0.0, 2.0, ALU.is_ge, ALU.mult)
+        nc.gpsimd.tensor_scalar(sign[:], twice[:], 1.0, -1.0, ALU.mult, ALU.add)
+        nc.gpsimd.tensor_tensor(ga_abs[:], ga_t[:], sign[:], ALU.mult)
+        nc.gpsimd.tensor_tensor(gb_signed[:], gb_t[:], sign[:], ALU.mult)
+
+        def gather_bytes(name, offsets, tag):
+            picked = keep.tile([P, S], U8, name=name, tag=tag, align_bytes=64)
+            nc.vector.tensor_copy(picked[:], plane[:].indirect(offsets[:]))
+            return picked
+
+        def gather_words(name, offsets):
+            picked = keep.tile([P, S], U32, name=name, align_bytes=64)
+            nc.vector.tensor_copy(picked[:], words[:].indirect(offsets[:]))
+            return picked
+
+        def deal(name, raw, tag, first=0, count=PACK):
+            grouped = keep.tile([P, count, P, PACK], BF16, name=name, tag=tag, align_bytes=64)
+            nc.scalar.copy(
+                out=grouped[:].rearrange("p t m j -> p m j t"),
+                in_=raw[:].rearrange("p j (m t) -> p m j t", t=PACK)[:, :, :, first : first + count],
+            )
+            return grouped
+
+        def quantize(name, grouped_flat):
+            width = grouped_flat.shape[1] // PACK
+            codes = keep.tile([P, width], U32, name=name + "_codes", align_bytes=64)
+            scales = keep.tile([P, width], U8, name=name + "_scales", align_bytes=64)
+            nc.vector.quantize_mx(out=codes[:].bitcast(FP8X4), scales=scales[:], in_=grouped_flat)
+            return codes, scales
+
+        def product(stationary, t, moving):
+            acc = psum.tile([P, S], F32, name="acc")
+            rows = slice(t * P, (t + 1) * P)
+            nc.tensor.matmul_mx(
+                out=acc[:],
+                lhsT=stationary[0][:, rows].bitcast(FP8X4),
+                lhsT_scale=stationary[1][:, rows],
+                rhs=moving[0][:].bitcast(FP8X4),
+                rhs_scale=moving[1][:],
+                start=True,
+                stop=True,
+            )
+            return acc
+
+        def emptied(name, acc, scale, width=S, tag=None):
+            tile = keep.tile([P, width], F32, name=name, tag=tag or name)
+            nc.scalar.activation(out=tile[:, :S], in_=acc[:], func=COPY, scale=scale)
+            return tile
+
+        flat = "p t m j -> p (t m j)"
+        c_three = gather_words("c_three", l_three)
+        c_offs = gather_words("c_offs", l_offs)
+        c_two = gather_words("c_two", l_two)
+        x_three = (c_three, gather_bytes("s_three", l_three, "s_three"))
+        b, late_bytes = [], []
+        for h, offsets in enumerate((l_offs, l_two)):
+            w3q = quantize(f"w3q{h}", deal(f"w3g{h}", raw3, f"w3g{h}", 2 * h, 2)[:].rearrange(flat))
+            b.extend(emptied(f"b{2 * h + u}", product(w3q, u, x_three), 1.0, 2 * V) for u in range(2))
+            late_bytes.append(gather_bytes(f"late_bytes{h}", offsets, f"w3g{h}"))
+        x_offs = (c_offs, late_bytes[0])
+        x_two = (c_two, late_bytes[1])
+        w1g = deal("w1g", raw1, "w3q1_codes")
+        w2g = deal("w2g", raw2, "w3q1_scales")
+
+        z2 = keep.tile([P, PACK, V], BF16, name="z2")
+        diffs = []
+        y, d = [], []
+
+        def finish_z2(t):
+            nc.vector.scalar_tensor_tensor(z2[:, t, :], diffs[t][:], gb_signed[:, t : t + 1], b[t][:, :V], ALU.mult, ALU.mult)
+
+        for t in range(PACK):
+            at6 = ring.tile([P, V], F32, name="at6")
+            diff = ring.tile([P, V], F32, name="diff")
+            diffs.append(diff)
+            nc.vector.tensor_copy(at6[:], b[t][:].indirect(l6[:]))
+            if t > 0:
+                finish_z2(t - 1)
+            nc.vector.tensor_tensor(diff[:], b[t][:].indirect(l5[:]), at6[:], ALU.subtract)
+            if t == 1:
+                w1q = quantize("w1q", w1g[:].rearrange(flat))
+                y = [emptied(f"y{u}", product(w1q, u, x_offs), ga_abs[:, u : u + 1], 2 * S) for u in range(PACK)]
+            if t == 2:
+                w2q = quantize("w2q", w2g[:].rearrange(flat))
+                d = [emptied(f"d{u}", product(w2q, u, x_two), ga_abs[:, u : u + 1], 2 * S) for u in range(PACK)]
+
+        z = keep.tile([P, PACK, S], BF16, name="z")
+        zg = keep.tile([P, PACK, P, PACK], BF16, name="zg", align_bytes=64)
+        z_codes = keep.tile([P, S], U32, name="z_codes", align_bytes=64)
+        z_scales = keep.tile([P, S], U8, name="z_scales", align_bytes=64)
+        z2g = keep.tile([P, V, PACK], BF16, name="z2g", align_bytes=64)
+        sums = {}
+
+        def finish_z(t, start, stop):
+            nc.vector.tensor_tensor(z[:, t, start:stop], sums[t, start][0], sums[t, start][1], ALU.max)
+
+        def deal_z(h, copy):
+            m = slice(h * P // 2, (h + 1) * P // 2)
+            copy(
+                out=zg[:, :, m, :].rearrange("p t m j -> p m j t"),
+                in_=z[:, :, cols(h)].rearrange("p j (m t) -> p m j t", t=PACK),
+            )
+
+        def quantize_z(h):
+            for t in range(PACK):
+                m = slice(h * P // 2, (h + 1) * P // 2)
+                c = slice(t * P + h * P // 2, t * P + (h + 1) * P // 2)
+                nc.vector.quantize_mx(
+                    out=z_codes[:, c].bitcast(FP8X4), scales=z_scales[:, c], in_=zg[:, t, m, :].rearrange("p m j -> p (m j)")
+                )
+
+        steps = [(t, 0, S) for t in range(PACK - 1)] + [(PACK - 1, 0, HALF), (PACK - 1, HALF, S)]
+        for i, (t, start, stop) in enumerate(steps):
+            at1 = ring.tile([P, stop - start], F32, name="at1")
+            at2 = ring.tile([P, stop - start], F32, name="at2")
+            first = ring.tile([P, stop - start], F32, name="first")
+            second = ring.tile([P, stop - start], F32, name="second")
+            sums[t, start] = (first[:], second[:])
+            entries = slice(start // STRIPE, stop // STRIPE)
+            nc.vector.tensor_copy(at1[:], y[t][:].indirect(l1[:, entries]))
+            nc.vector.tensor_copy(at2[:], y[t][:].indirect(l2[:, entries]))
+            if i == 0:
+                finish_z2(PACK - 1)
+                nc.scalar.copy(
+                    out=z2g[:].rearrange("p (c i) j -> p c j i", i=PACK), in_=z2[:].rearrange("p j (c i) -> p c j i", i=PACK)
+                )
+            else:
+                finish_z(*steps[i - 1])
+            if i == PACK:
+                deal_z(0, nc.scalar.copy)
+            nc.vector.tensor_tensor(first[:], d[t][:].indirect(l3[:, entries]), at1[:], ALU.add)
+            nc.vector.tensor_tensor(second[:], d[t][:].indirect(l4[:, entries]), at2[:], ALU.add)
+            if i == 1:
+                z2q = quantize("z2q", z2g[:].rearrange("p v j -> p (v j)"))
+        finish_z(*steps[-1])
+        quantize_z(0)
+        deal_z(1, nc.vector.tensor_copy)
+        quantize_z(1)
+
+        minus, plus = [], []
+        for t in range(PACK):
+            acc = product((z_codes, z_scales), t, z2q)
+            minus.append(emptied(f"minus{t}", acc, -0.0625, 2 * V, f"b{t}"))
+            plus.append(emptied(f"plus{t}", acc, 0.0625))
+        st = [keep.tile([P, 2 * V], F32, name=f"st{t}", tag=f"y{t}") for t in range(PACK)]
+        at8 = [keep.tile([P, V], F32, name=f"at8_{t}") for t in range(PACK)]
+        su = [keep.tile([P, V], F32, name=f"su{t}") for t in range(PACK)]
+        su_half = [keep.tile([P, 2 * V], F32, name=f"su_half{t}", tag=f"d{t}") for t in range(PACK)]
+        result = [keep.tile([P, V], F32, name=f"result{t}") for t in range(PACK)]
+        out_rows = out.rearrange("(p t) v -> p t v", t=PACK)
+
+        def stage7(t):
+            nc.vector.tensor_tensor(st[t][:, :V], minus[t][:].indirect(l7[:]), plus[t][:], ALU.add)
+
+        def stage8(t):
+            nc.vector.tensor_copy(at8[t][:], st[t][:].indirect(l8[:]))
+
+        def larger(t):
+            nc.vector.tensor_tensor(su[t][:], st[t][:, :V], at8[t][:], ALU.max)
+            nc.scalar.activation(out=su_half[t][:, :V], in_=su[t][:], func=COPY, scale=0.5)
+
+        def stage9(t):
+            if t < PACK - 1:
+                nc.vector.tensor_tensor(result[t][:], su_half[t][:].indirect(l9[:]), su[t][:], ALU.add)
+                nc.sync.dma_start(out=out_rows[:, t, :], in_=result[t][:])
+                return
+            for h in range(2):
+                nc.vector.tensor_tensor(result[t][:, cols(h)], su_half[t][:].indirect(half_of(l9, h)), su[t][:, cols(h)], ALU.add)
+                nc.sync.dma_start(out=out_rows[:, t, cols(h)], in_=result[t][:, cols(h)])
+
+        stages = [stage7, stage8, larger, stage9]
+        for wave in range(PACK + len(stages) - 1):
+            for i, stage in enumerate(stages):
+                if 0 <= wave - i < PACK:
+                    stage(wave - i)

@@ -1,6 +1,7 @@
 from contextlib import ExitStack
 
 import concourse.mybir as mybir
+from concourse.masks import make_identity
 
 K, T, S, V, H = 512, 2048, 512, 512, 512
 FLOPS = 2 * K * H * (S + S + V) + 2 * H * S * V
@@ -14,6 +15,7 @@ U8 = mybir.dt.uint8
 FP8X4 = mybir.dt.float8_e4m3fn_x4
 ALU = mybir.AluOpType
 COPY = mybir.ActivationFunctionType.Copy
+RELU = mybir.ActivationFunctionType.Relu
 
 P = 128
 PACK = 4
@@ -28,8 +30,9 @@ def tile_picked_twkpathbwindthree_none_p_kernel(
     with ExitStack() as ctx:
         lists = ctx.enter_context(tc.tile_pool(name="lists", bufs=1))
         keep = ctx.enter_context(tc.tile_pool(name="keep", bufs=1))
-        ring = ctx.enter_context(tc.tile_pool(name="ring", bufs=3))
-        psum = ctx.enter_context(tc.psum_pool(name="psum", bufs=8))
+        ring = ctx.enter_context(tc.tile_pool(name="ring", bufs=2))
+        psum = ctx.enter_context(tc.psum_pool(name="psum", bufs=4))
+        zbank = ctx.enter_context(tc.psum_pool(name="zbank", bufs=1))
 
         def load_list(name, src):
             tile = lists.tile([P, S // STRIPE], U16, name=name)
@@ -49,22 +52,22 @@ def tile_picked_twkpathbwindthree_none_p_kernel(
 
         plane = keep.tile([P, T], U8, name="plane", align_bytes=64)
         nc.vector.memset(plane[:].bitcast(I32), 0)
-        l_three = load_list("l_three", three)
+        l_offs = load_list("l_offs", offs)
         for q in range(4):
             nc.scalar.dma_start(out=plane[32 * q : 32 * q + 4, :].bitcast(I32), in_=x_scales[0, 4 * q : 4 * q + 4, :].bitcast(I32))
         words = keep.tile([P, T], U32, name="words", align_bytes=64)
         nc.sync.dma_start(out=words[:].bitcast(I32), in_=x_words[0].rearrange("p n t -> p (n t)").bitcast(I32))
-        l_offs = load_list("l_offs", offs)
         l_two = load_list("l_two", two)
-        raw3 = load_weight("raw3", w3)
-        l5 = load_list("l5", n5)
-        l6 = load_list("l6", n6)
+        l_three = load_list("l_three", three)
         raw1 = load_weight("raw1", w1)
         raw2 = load_weight("raw2", w2)
         l1 = load_list("l1", n1)
-        l2 = load_list("l2", n2)
         l3 = load_list("l3", n3)
+        raw3 = load_weight("raw3", w3)
+        l2 = load_list("l2", n2)
         l4 = load_list("l4", n4)
+        l6 = load_list("l6", n6)
+        l5 = load_list("l5", n5)
         l7 = load_list("l7", n7)
         l8 = load_list("l8", n8)
         l9 = load_list("l9", n9)
@@ -85,12 +88,12 @@ def tile_picked_twkpathbwindthree_none_p_kernel(
         def gather_bytes(name, offsets, tag):
             picked = keep.tile([P, S], U8, name=name, tag=tag, align_bytes=64)
             nc.vector.tensor_copy(picked[:], plane[:].indirect(offsets[:]))
-            return picked
+            return picked[:]
 
         def gather_words(name, offsets):
             picked = keep.tile([P, S], U32, name=name, align_bytes=64)
             nc.vector.tensor_copy(picked[:], words[:].indirect(offsets[:]))
-            return picked
+            return picked[:]
 
         def deal(name, raw, tag, first=0, count=PACK):
             grouped = keep.tile([P, count, P, PACK], BF16, name=name, tag=tag, align_bytes=64)
@@ -107,15 +110,18 @@ def tile_picked_twkpathbwindthree_none_p_kernel(
             nc.vector.quantize_mx(out=codes[:].bitcast(FP8X4), scales=scales[:], in_=grouped_flat)
             return codes, scales
 
-        def product(stationary, t, moving):
-            acc = psum.tile([P, S], F32, name="acc")
+        def product(stationary, t, moving, spare_bank=False):
+            if spare_bank:
+                acc = zbank.tile([P, moving[1].shape[1]], F32, name=f"turned{t}")
+            else:
+                acc = psum.tile([P, moving[1].shape[1]], F32, name="acc")
             rows = slice(t * P, (t + 1) * P)
             nc.tensor.matmul_mx(
                 out=acc[:],
                 lhsT=stationary[0][:, rows].bitcast(FP8X4),
                 lhsT_scale=stationary[1][:, rows],
-                rhs=moving[0][:].bitcast(FP8X4),
-                rhs_scale=moving[1][:],
+                rhs=moving[0].bitcast(FP8X4),
+                rhs_scale=moving[1],
                 start=True,
                 stop=True,
             )
@@ -127,109 +133,150 @@ def tile_picked_twkpathbwindthree_none_p_kernel(
             return tile
 
         flat = "p t m j -> p (t m j)"
-        c_three = gather_words("c_three", l_three)
+        ident = keep.tile([P, P], F32, name="ident")
+        make_identity(nc, ident[:])
+
+        def project(name, wq, first, moving, scales, widths=(2 * S,) * PACK):
+            return [
+                emptied(f"{name}{first + u}", product(wq, u, moving), scales[first + u], widths[first + u])
+                for u in range(wq[1].shape[1] // P)
+            ]
+
+        gains = [ga_abs[:, t : t + 1] for t in range(PACK)]
         c_offs = gather_words("c_offs", l_offs)
         c_two = gather_words("c_two", l_two)
-        x_three = (c_three, gather_bytes("s_three", l_three, "s_three"))
-        b, late_bytes = [], []
-        for h, offsets in enumerate((l_offs, l_two)):
-            w3q = quantize(f"w3q{h}", deal(f"w3g{h}", raw3, f"w3g{h}", 2 * h, 2)[:].rearrange(flat))
-            b.extend(emptied(f"b{2 * h + u}", product(w3q, u, x_three), 1.0, 2 * V) for u in range(2))
-            late_bytes.append(gather_bytes(f"late_bytes{h}", offsets, f"w3g{h}"))
-        x_offs = (c_offs, late_bytes[0])
-        x_two = (c_two, late_bytes[1])
-        w1g = deal("w1g", raw1, "w3q1_codes")
-        w2g = deal("w2g", raw2, "w3q1_scales")
+        c_three = gather_words("c_three", l_three)
+        x_offs = (c_offs, gather_bytes("s_offs", l_offs, "s_offs"))
+        y, d, late_bytes = [], [], []
+        for h, offsets in enumerate((l_two, l_three)):
+            w1q = quantize(f"w1q{h}", deal(f"w1g{h}", raw1, f"w1g{h}", 2 * h, 2)[:].rearrange(flat))
+            y.extend(project("y", w1q, 2 * h, x_offs, gains))
+            late_bytes.append(gather_bytes(f"late_bytes{h}", offsets, f"w1g{h}"))
+        x_two = (c_two, late_bytes[0])
+        x_three = (c_three, late_bytes[1])
+
+        at1 = []
+        for t in range(PACK):
+            if t >= 2:
+                h = t - 2
+                w2q = quantize(f"w2q{h}", deal(f"w2g{h}", raw2, f"w1q{h}_codes", 2 * h, 2)[:].rearrange(flat))
+                d.extend(project("d", w2q, 2 * h, x_two, gains))
+            tile = keep.tile([P, S], F32, name=f"at1_{t}", tag=f"w1q{t - 2}_codes" if t >= 2 else f"at1_{t}", align_bytes=64)
+            nc.vector.tensor_copy(tile[:], y[t][:].indirect(l1[:]))
+            at1.append(tile)
+
+        turned = [zbank.tile([P, PACK, P], F32, name=f"turned{c}") for c in range(PACK)]
+        b = []
+        for pair in ((0, 1), (2, 3)):
+            if pair[0] == 2:
+                w3q = quantize("w3q", deal("w3g", raw3, "w2q1_codes")[:].rearrange(flat))
+                b = project("b", w3q, 0, x_three, [1.0] * PACK, (2 * V, 2 * V, 2 * V, V))
+            first, part, excess = {}, {}, {}
+            for t in pair:
+                first[t] = keep.tile([P, S], F32, name=f"first{t}", tag="w2q1_codes" if t == 2 else f"first{t}", align_bytes=64)
+                nc.vector.tensor_tensor(first[t][:], d[t][:].indirect(l3[:]), at1[t][:], ALU.add)
+            for t in pair:
+                part[t] = ring.tile([P, S], F32, name="part")
+                nc.vector.tensor_tensor(part[t][:], y[t][:].indirect(l2[:]), first[t][:], ALU.subtract)
+            for t in pair:
+                excess[t] = ring.tile([P, S], F32, name="excess")
+                nc.vector.tensor_tensor(excess[t][:], d[t][:].indirect(l4[:]), part[t][:], ALU.add)
+                gain = ring.tile([P, S], F32, name="gain")
+                nc.scalar.activation(out=gain[:], in_=excess[t][:], func=RELU)
+                for c in range(PACK):
+                    places = slice(c * P, (c + 1) * P)
+                    nc.tensor.matmul(turned[c][:, t, :], gain[:, places], ident[:], start=True, stop=False, is_transpose=True)
+                    nc.tensor.matmul(turned[c][:, t, :], first[t][:, places], ident[:], start=False, stop=True, is_transpose=True)
+
+        zg = keep.tile([P, PACK, P, PACK], BF16, name="zg", align_bytes=64)
+        zg_words = zg[:].rearrange(flat).bitcast(F32).rearrange("p (t m u) -> p t m u", t=PACK, u=2)
+        for c in range(PACK):
+            rounded = ring.tile([P, 2, P, 2], BF16, name="rounded")
+            nc.scalar.copy(out=rounded[:], in_=turned[c][:].rearrange("n (u e) p -> n u p e", e=2))
+            pairs = rounded[:].rearrange("n u p e -> n (u p e)").bitcast(F32)
+            back = psum.tile([P, 2, P], F32, name="acc")
+            for u in range(2):
+                nc.tensor.transpose(back[:, u, :], pairs[:, u * P : (u + 1) * P], ident[:])
+            m = slice(c * P // PACK, (c + 1) * P // PACK)
+            nc.scalar.copy(out=zg_words[:, :, m, :], in_=back[:].rearrange("p u (m t) -> p t m u", t=PACK))
 
         z2 = keep.tile([P, PACK, V], BF16, name="z2")
-        diffs = []
-        y, d = [], []
-
-        def finish_z2(t):
-            nc.vector.scalar_tensor_tensor(z2[:, t, :], diffs[t][:], gb_signed[:, t : t + 1], b[t][:, :V], ALU.mult, ALU.mult)
-
-        for t in range(PACK):
-            at6 = ring.tile([P, V], F32, name="at6")
-            diff = ring.tile([P, V], F32, name="diff")
-            diffs.append(diff)
-            nc.vector.tensor_copy(at6[:], b[t][:].indirect(l6[:]))
-            if t > 0:
-                finish_z2(t - 1)
-            nc.vector.tensor_tensor(diff[:], b[t][:].indirect(l5[:]), at6[:], ALU.subtract)
-            if t == 1:
-                w1q = quantize("w1q", w1g[:].rearrange(flat))
-                y = [emptied(f"y{u}", product(w1q, u, x_offs), ga_abs[:, u : u + 1], 2 * S) for u in range(PACK)]
-            if t == 2:
-                w2q = quantize("w2q", w2g[:].rearrange(flat))
-                d = [emptied(f"d{u}", product(w2q, u, x_two), ga_abs[:, u : u + 1], 2 * S) for u in range(PACK)]
-
-        z = keep.tile([P, PACK, S], BF16, name="z")
-        zg = keep.tile([P, PACK, P, PACK], BF16, name="zg", align_bytes=64)
-        z_codes = keep.tile([P, S], U32, name="z_codes", align_bytes=64)
-        z_scales = keep.tile([P, S], U8, name="z_scales", align_bytes=64)
         z2g = keep.tile([P, V, PACK], BF16, name="z2g", align_bytes=64)
-        sums = {}
+        diffs = {}
 
-        def finish_z(t, start, stop):
-            nc.vector.tensor_tensor(z[:, t, start:stop], sums[t, start][0], sums[t, start][1], ALU.max)
-
-        def deal_z(h, copy):
-            m = slice(h * P // 2, (h + 1) * P // 2)
-            copy(
-                out=zg[:, :, m, :].rearrange("p t m j -> p m j t"),
-                in_=z[:, :, cols(h)].rearrange("p j (m t) -> p m j t", t=PACK),
+        def finish_z2(t, start, stop):
+            nc.vector.scalar_tensor_tensor(
+                z2[:, t, start:stop], diffs[t, start][:], gb_signed[:, t : t + 1], b[t][:, start:stop], ALU.mult, ALU.mult
             )
 
-        def quantize_z(h):
-            for t in range(PACK):
-                m = slice(h * P // 2, (h + 1) * P // 2)
-                c = slice(t * P + h * P // 2, t * P + (h + 1) * P // 2)
-                nc.vector.quantize_mx(
-                    out=z_codes[:, c].bitcast(FP8X4), scales=z_scales[:, c], in_=zg[:, t, m, :].rearrange("p m j -> p (m j)")
-                )
+        def weave_z2(start, stop, copy):
+            copy(
+                out=z2g[:, start:stop, :].rearrange("p (c i) j -> p c j i", i=PACK),
+                in_=z2[:, :, start:stop].rearrange("p j (c i) -> p c j i", i=PACK),
+            )
 
-        steps = [(t, 0, S) for t in range(PACK - 1)] + [(PACK - 1, 0, HALF), (PACK - 1, HALF, S)]
-        for i, (t, start, stop) in enumerate(steps):
-            at1 = ring.tile([P, stop - start], F32, name="at1")
-            at2 = ring.tile([P, stop - start], F32, name="at2")
-            first = ring.tile([P, stop - start], F32, name="first")
-            second = ring.tile([P, stop - start], F32, name="second")
-            sums[t, start] = (first[:], second[:])
-            entries = slice(start // STRIPE, stop // STRIPE)
-            nc.vector.tensor_copy(at1[:], y[t][:].indirect(l1[:, entries]))
-            nc.vector.tensor_copy(at2[:], y[t][:].indirect(l2[:, entries]))
-            if i == 0:
-                finish_z2(PACK - 1)
-                nc.scalar.copy(
-                    out=z2g[:].rearrange("p (c i) j -> p c j i", i=PACK), in_=z2[:].rearrange("p j (c i) -> p c j i", i=PACK)
-                )
-            else:
-                finish_z(*steps[i - 1])
-            if i == PACK:
-                deal_z(0, nc.scalar.copy)
-            nc.vector.tensor_tensor(first[:], d[t][:].indirect(l3[:, entries]), at1[:], ALU.add)
-            nc.vector.tensor_tensor(second[:], d[t][:].indirect(l4[:, entries]), at2[:], ALU.add)
-            if i == 1:
-                z2q = quantize("z2q", z2g[:].rearrange("p v j -> p (v j)"))
-        finish_z(*steps[-1])
-        quantize_z(0)
-        deal_z(1, nc.vector.tensor_copy)
-        quantize_z(1)
+        last = PACK - 1
+        for t in range(last):
+            at6 = ring.tile([P, V], F32, name="at6")
+            nc.vector.tensor_copy(at6[:], b[t][:].indirect(l6[:]))
+            if t > 0:
+                finish_z2(t - 1, 0, V)
+            diffs[t, 0] = ring.tile([P, V], F32, name="diff")
+            nc.vector.tensor_tensor(diffs[t, 0][:], b[t][:].indirect(l5[:]), at6[:], ALU.subtract)
+        zq = quantize("zq", zg[:].rearrange(flat))
+        at6 = keep.tile([P, V], F32, name="at6_last", tag="zg", align_bytes=64)
+        for h in range(2):
+            nc.vector.tensor_copy(at6[:, cols(h)], b[last][:].indirect(half_of(l6, h)))
+        finish_z2(last - 1, 0, V)
+        pieces = [(0, HALF), (HALF, HALF + P), (HALF + P, V)]
+        for i, (start, stop) in enumerate(pieces):
+            diffs[last, start] = ring.tile([P, stop - start], F32, name="diff")
+            entries = l5[:, start // STRIPE : stop // STRIPE]
+            nc.vector.tensor_tensor(diffs[last, start][:], b[last][:].indirect(entries), at6[:, start:stop], ALU.subtract)
+            if i > 0:
+                finish_z2(last, *pieces[i - 1])
+                weave_z2(*pieces[i - 1], nc.scalar.copy)
+        finish_z2(last, *pieces[-1])
+        z2_codes = keep.tile([P, V], U32, name="z2_codes", align_bytes=64)
+        z2_scales = keep.tile([P, V], U8, name="z2_scales", align_bytes=64)
+
+        def quantize_z2(start, stop):
+            nc.vector.quantize_mx(
+                out=z2_codes[:, start:stop].bitcast(FP8X4),
+                scales=z2_scales[:, start:stop],
+                in_=z2g[:, start:stop, :].rearrange("p v j -> p (v j)"),
+            )
+
+        quantize_z2(*pieces[0])
+        weave_z2(*pieces[-1], nc.vector.tensor_copy)
+        for piece in pieces[1:]:
+            quantize_z2(*piece)
 
         minus, plus = [], []
         for t in range(PACK):
-            acc = product((z_codes, z_scales), t, z2q)
-            minus.append(emptied(f"minus{t}", acc, -0.0625, 2 * V, f"b{t}"))
-            plus.append(emptied(f"plus{t}", acc, 0.0625))
-        st = [keep.tile([P, 2 * V], F32, name=f"st{t}", tag=f"y{t}") for t in range(PACK)]
+            minus.append(keep.tile([P, 2 * V], F32, name=f"minus{t}", tag=f"y{t}"))
+            plus.append(keep.tile([P, V], F32, name=f"plus{t}"))
+            cuts = pieces if t == 0 else [(0, V)]
+            accs = [product(zq, t, (z2_codes[:, start:stop], z2_scales[:, start:stop]), t > 0) for start, stop in cuts]
+            for acc, (start, stop) in zip(accs, cuts):
+                nc.scalar.activation(out=minus[t][:, start:stop], in_=acc[:], func=COPY, scale=-0.0625)
+                if start == 0:
+                    nc.scalar.activation(out=plus[t][:, start:stop], in_=acc[:], func=COPY, scale=0.0625)
+            for acc, (start, stop) in list(zip(accs, cuts))[1:]:
+                nc.scalar.activation(out=plus[t][:, start:stop], in_=acc[:], func=COPY, scale=0.0625)
+        st = [keep.tile([P, 2 * V], F32, name=f"st{t}", tag=f"d{t}") for t in range(PACK)]
         at8 = [keep.tile([P, V], F32, name=f"at8_{t}") for t in range(PACK)]
         su = [keep.tile([P, V], F32, name=f"su{t}") for t in range(PACK)]
-        su_half = [keep.tile([P, 2 * V], F32, name=f"su_half{t}", tag=f"d{t}") for t in range(PACK)]
+        su_half = [keep.tile([P, 2 * V], F32, name=f"su_half{t}", tag=f"b{t}") for t in range(PACK)]
         result = [keep.tile([P, V], F32, name=f"result{t}") for t in range(PACK)]
         out_rows = out.rearrange("(p t) v -> p t v", t=PACK)
 
         def stage7(t):
-            nc.vector.tensor_tensor(st[t][:, :V], minus[t][:].indirect(l7[:]), plus[t][:], ALU.add)
+            if t > 0:
+                nc.vector.tensor_tensor(st[t][:, :V], minus[t][:].indirect(l7[:]), plus[t][:], ALU.add)
+                return
+            for h in range(2):
+                nc.vector.tensor_tensor(st[t][:, cols(h)], minus[t][:].indirect(half_of(l7, h)), plus[t][:, cols(h)], ALU.add)
 
         def stage8(t):
             nc.vector.tensor_copy(at8[t][:], st[t][:].indirect(l8[:]))

@@ -83,6 +83,8 @@ def tile_picked_twkpathbwindthree_none_p_kernel(
         nc.gpsimd.tensor_scalar(twice[:], ga_t[:], 0.0, 2.0, ALU.is_ge, ALU.mult)
         nc.gpsimd.tensor_scalar(sign[:], twice[:], 1.0, -1.0, ALU.mult, ALU.add)
         nc.gpsimd.tensor_tensor(ga_abs[:], ga_t[:], sign[:], ALU.mult)
+        ga_minus = keep.tile([P, PACK], F32, name="ga_minus")
+        nc.gpsimd.tensor_scalar(ga_minus[:], ga_abs[:], -1.0, 0.0, ALU.mult, ALU.add)
         nc.gpsimd.tensor_tensor(gb_signed[:], gb_t[:], sign[:], ALU.mult)
 
         def gather_bytes(name, offsets, tag):
@@ -136,69 +138,71 @@ def tile_picked_twkpathbwindthree_none_p_kernel(
         ident = keep.tile([P, P], F32, name="ident")
         make_identity(nc, ident[:])
 
-        def project(name, wq, first, moving, scales, widths=(2 * S,) * PACK):
-            return [
-                emptied(f"{name}{first + u}", product(wq, u, moving), scales[first + u], widths[first + u])
-                for u in range(wq[1].shape[1] // P)
-            ]
+        def project_both(plain, negated, wq, moving):
+            for u in range(2):
+                t = len(plain)
+                acc = product(wq, u, moving)
+                plain.append(emptied("plain", acc, ga_abs[:, t : t + 1], 2 * S, f"y{t}"))
+                negated.append(emptied("negated", acc, ga_minus[:, t : t + 1], 2 * S, f"d{t}"))
 
-        gains = [ga_abs[:, t : t + 1] for t in range(PACK)]
         c_offs = gather_words("c_offs", l_offs)
         c_two = gather_words("c_two", l_two)
         c_three = gather_words("c_three", l_three)
         x_offs = (c_offs, gather_bytes("s_offs", l_offs, "s_offs"))
-        y, d, late_bytes = [], [], []
+        y, minus_y, late_bytes = [], [], []
         for h, offsets in enumerate((l_two, l_three)):
             w1q = quantize(f"w1q{h}", deal(f"w1g{h}", raw1, f"w1g{h}", 2 * h, 2)[:].rearrange(flat))
-            y.extend(project("y", w1q, 2 * h, x_offs, gains))
+            project_both(y, minus_y, w1q, x_offs)
             late_bytes.append(gather_bytes(f"late_bytes{h}", offsets, f"w1g{h}"))
         x_two = (c_two, late_bytes[0])
         x_three = (c_three, late_bytes[1])
 
-        at1 = []
+        at1, at2 = [], []
+        d, minus_d = [], []
         for t in range(PACK):
             if t >= 2:
                 h = t - 2
                 w2q = quantize(f"w2q{h}", deal(f"w2g{h}", raw2, f"w1q{h}_codes", 2 * h, 2)[:].rearrange(flat))
-                d.extend(project("d", w2q, 2 * h, x_two, gains))
-            tile = keep.tile([P, S], F32, name=f"at1_{t}", tag=f"w1q{t - 2}_codes" if t >= 2 else f"at1_{t}", align_bytes=64)
-            nc.vector.tensor_copy(tile[:], y[t][:].indirect(l1[:]))
-            at1.append(tile)
+            at1.append(keep.tile([P, S], F32, name=f"at1_{t}", tag=f"w1q{t - 2}_codes" if t >= 2 else f"at1_{t}", align_bytes=64))
+            at2.append(keep.tile([P, S], F32, name=f"at2_{t}"))
+            nc.vector.tensor_copy(at1[t][:], y[t][:].indirect(l1[:]))
+            nc.vector.tensor_copy(at2[t][:], minus_y[t][:].indirect(l2[:]))
+            if t >= 2:
+                project_both(d, minus_d, w2q, x_two)
 
-        turned = [zbank.tile([P, PACK, P], F32, name=f"turned{c}") for c in range(PACK)]
-        b = []
-        for pair in ((0, 1), (2, 3)):
-            if pair[0] == 2:
+        def turn_and_add(bank, terms):
+            for i, term in enumerate(terms):
+                nc.tensor.matmul(bank, term, ident[:], start=i == 0, stop=i == len(terms) - 1, is_transpose=True)
+
+        larger_sum = [zbank.tile([P, PACK, P], F32, name=f"turned{c}") for c in range(PACK)]
+        for t in range(PACK):
+            if t == 2:
                 w3q = quantize("w3q", deal("w3g", raw3, "w2q1_codes")[:].rearrange(flat))
-                b = project("b", w3q, 0, x_three, [1.0] * PACK, (2 * V, 2 * V, 2 * V, V))
-            first, part, excess = {}, {}, {}
-            for t in pair:
-                first[t] = keep.tile([P, S], F32, name=f"first{t}", tag="w2q1_codes" if t == 2 else f"first{t}", align_bytes=64)
-                nc.vector.tensor_tensor(first[t][:], d[t][:].indirect(l3[:]), at1[t][:], ALU.add)
-            for t in pair:
-                part[t] = ring.tile([P, S], F32, name="part")
-                nc.vector.tensor_tensor(part[t][:], y[t][:].indirect(l2[:]), first[t][:], ALU.subtract)
-            for t in pair:
-                excess[t] = ring.tile([P, S], F32, name="excess")
-                nc.vector.tensor_tensor(excess[t][:], d[t][:].indirect(l4[:]), part[t][:], ALU.add)
-                gain = ring.tile([P, S], F32, name="gain")
-                nc.scalar.activation(out=gain[:], in_=excess[t][:], func=RELU)
-                for c in range(PACK):
-                    places = slice(c * P, (c + 1) * P)
-                    nc.tensor.matmul(turned[c][:, t, :], gain[:, places], ident[:], start=True, stop=False, is_transpose=True)
-                    nc.tensor.matmul(turned[c][:, t, :], first[t][:, places], ident[:], start=False, stop=True, is_transpose=True)
+                b = [emptied(f"b{u}", product(w3q, u, x_three), 1.0, V if u == PACK - 1 else 2 * V) for u in range(PACK)]
+                at3 = keep.tile([P, S], F32, name="at3_held", tag="w2q1_codes", align_bytes=64)
+            else:
+                at3 = ring.tile([P, S], F32, name="at3")
+            at4 = ring.tile([P, S], F32, name="at4")
+            nc.vector.tensor_copy(at3[:], d[t][:].indirect(l3[:]))
+            nc.vector.tensor_copy(at4[:], minus_d[t][:].indirect(l4[:]))
+            first_bank = psum.tile([P, PACK, P], F32, name="acc")
+            lead_bank = psum.tile([P, PACK, P], F32, name="acc")
+            blocks = [slice(c * P, (c + 1) * P) for c in range(PACK)]
+            for c in range(PACK):
+                turn_and_add(first_bank[:, c, :], [at1[t][:, blocks[c]], at3[:, blocks[c]]])
+            for c in range(PACK):
+                turn_and_add(lead_bank[:, c, :], [term[:, blocks[c]] for term in (at1[t], at2[t], at3, at4)])
+            first = ring.tile([P, PACK, P], F32, name="first")
+            gain = ring.tile([P, PACK, P], F32, name="gain")
+            nc.scalar.activation(out=first[:], in_=first_bank[:], func=COPY)
+            nc.scalar.activation(out=gain[:], in_=lead_bank[:], func=RELU, scale=-1.0)
+            for c in range(PACK):
+                turn_and_add(larger_sum[c][:, t, :], [first[:, c, :], gain[:, c, :]])
 
         zg = keep.tile([P, PACK, P, PACK], BF16, name="zg", align_bytes=64)
-        zg_words = zg[:].rearrange(flat).bitcast(F32).rearrange("p (t m u) -> p t m u", t=PACK, u=2)
         for c in range(PACK):
-            rounded = ring.tile([P, 2, P, 2], BF16, name="rounded")
-            nc.scalar.copy(out=rounded[:], in_=turned[c][:].rearrange("n (u e) p -> n u p e", e=2))
-            pairs = rounded[:].rearrange("n u p e -> n (u p e)").bitcast(F32)
-            back = psum.tile([P, 2, P], F32, name="acc")
-            for u in range(2):
-                nc.tensor.transpose(back[:, u, :], pairs[:, u * P : (u + 1) * P], ident[:])
             m = slice(c * P // PACK, (c + 1) * P // PACK)
-            nc.scalar.copy(out=zg_words[:, :, m, :], in_=back[:].rearrange("p u (m t) -> p t m u", t=PACK))
+            nc.scalar.copy(out=zg[:, :, m, :], in_=larger_sum[c][:].rearrange("p j (m t) -> p t m j", t=PACK))
 
         z2 = keep.tile([P, PACK, V], BF16, name="z2")
         z2g = keep.tile([P, V, PACK], BF16, name="z2g", align_bytes=64)

@@ -31,8 +31,7 @@ def tile_picked_twkpathbwindthree_none_p_kernel(
         lists = ctx.enter_context(tc.tile_pool(name="lists", bufs=1))
         keep = ctx.enter_context(tc.tile_pool(name="keep", bufs=1))
         ring = ctx.enter_context(tc.tile_pool(name="ring", bufs=2))
-        psum = ctx.enter_context(tc.psum_pool(name="psum", bufs=4))
-        zbank = ctx.enter_context(tc.psum_pool(name="zbank", bufs=1))
+        psum = ctx.enter_context(tc.psum_pool(name="psum", bufs=8))
 
         def load_list(name, src):
             tile = lists.tile([P, S // STRIPE], U16, name=name)
@@ -112,11 +111,8 @@ def tile_picked_twkpathbwindthree_none_p_kernel(
             nc.vector.quantize_mx(out=codes[:].bitcast(FP8X4), scales=scales[:], in_=grouped_flat)
             return codes, scales
 
-        def product(stationary, t, moving, spare_bank=False):
-            if spare_bank:
-                acc = zbank.tile([P, moving[1].shape[1]], F32, name=f"turned{t}")
-            else:
-                acc = psum.tile([P, moving[1].shape[1]], F32, name="acc")
+        def product(stationary, t, moving):
+            acc = psum.tile([P, moving[1].shape[1]], F32, name="acc")
             rows = slice(t * P, (t + 1) * P)
             nc.tensor.matmul_mx(
                 out=acc[:],
@@ -138,71 +134,82 @@ def tile_picked_twkpathbwindthree_none_p_kernel(
         ident = keep.tile([P, P], F32, name="ident")
         make_identity(nc, ident[:])
 
-        def project_both(plain, negated, wq, moving):
-            for u in range(2):
-                t = len(plain)
-                acc = product(wq, u, moving)
-                plain.append(emptied("plain", acc, ga_abs[:, t : t + 1], 2 * S, f"y{t}"))
-                negated.append(emptied("negated", acc, ga_minus[:, t : t + 1], 2 * S, f"d{t}"))
-
-        c_offs = gather_words("c_offs", l_offs)
-        c_two = gather_words("c_two", l_two)
-        c_three = gather_words("c_three", l_three)
-        x_offs = (c_offs, gather_bytes("s_offs", l_offs, "s_offs"))
-        y, minus_y, late_bytes = [], [], []
-        for h, offsets in enumerate((l_two, l_three)):
-            w1q = quantize(f"w1q{h}", deal(f"w1g{h}", raw1, f"w1g{h}", 2 * h, 2)[:].rearrange(flat))
-            project_both(y, minus_y, w1q, x_offs)
-            late_bytes.append(gather_bytes(f"late_bytes{h}", offsets, f"w1g{h}"))
-        x_two = (c_two, late_bytes[0])
-        x_three = (c_three, late_bytes[1])
-
-        at1, at2 = [], []
-        d, minus_d = [], []
-        for t in range(PACK):
-            if t >= 2:
-                h = t - 2
-                w2q = quantize(f"w2q{h}", deal(f"w2g{h}", raw2, f"w1q{h}_codes", 2 * h, 2)[:].rearrange(flat))
-            at1.append(keep.tile([P, S], F32, name=f"at1_{t}", tag=f"w1q{t - 2}_codes" if t >= 2 else f"at1_{t}", align_bytes=64))
-            at2.append(keep.tile([P, S], F32, name=f"at2_{t}"))
-            nc.vector.tensor_copy(at1[t][:], y[t][:].indirect(l1[:]))
-            nc.vector.tensor_copy(at2[t][:], minus_y[t][:].indirect(l2[:]))
-            if t >= 2:
-                project_both(d, minus_d, w2q, x_two)
+        def signed_pair(wq, u, moving, t, tags):
+            acc = product(wq, u, moving)
+            return (
+                emptied("plain", acc, ga_abs[:, t : t + 1], 2 * S, tags[0]),
+                emptied("negated", acc, ga_minus[:, t : t + 1], 2 * S, tags[1]),
+            )
 
         def turn_and_add(bank, terms):
             for i, term in enumerate(terms):
                 nc.tensor.matmul(bank, term, ident[:], start=i == 0, stop=i == len(terms) - 1, is_transpose=True)
 
-        larger_sum = [zbank.tile([P, PACK, P], F32, name=f"turned{c}") for c in range(PACK)]
-        for t in range(PACK):
-            if t == 2:
-                w3q = quantize("w3q", deal("w3g", raw3, "w2q1_codes")[:].rearrange(flat))
-                b = [emptied(f"b{u}", product(w3q, u, x_three), 1.0, V if u == PACK - 1 else 2 * V) for u in range(PACK)]
-                at3 = keep.tile([P, S], F32, name="at3_held", tag="w2q1_codes", align_bytes=64)
-            else:
-                at3 = ring.tile([P, S], F32, name="at3")
-            at4 = ring.tile([P, S], F32, name="at4")
-            nc.vector.tensor_copy(at3[:], d[t][:].indirect(l3[:]))
-            nc.vector.tensor_copy(at4[:], minus_d[t][:].indirect(l4[:]))
+        def fetch(name, window, offsets, tag=None):
+            tile = keep.tile([P, S], F32, name=name, tag=tag or name, align_bytes=64)
+            nc.vector.tensor_copy(tile[:], window[:].indirect(offsets[:]))
+            return tile
+
+        z = keep.tile([P, PACK, S], BF16, name="z")
+
+        def larger_on_tensor(t, y1, minus_y2, d3, minus_d4):
             first_bank = psum.tile([P, PACK, P], F32, name="acc")
             lead_bank = psum.tile([P, PACK, P], F32, name="acc")
             blocks = [slice(c * P, (c + 1) * P) for c in range(PACK)]
             for c in range(PACK):
-                turn_and_add(first_bank[:, c, :], [at1[t][:, blocks[c]], at3[:, blocks[c]]])
+                turn_and_add(first_bank[:, c, :], [y1[:, blocks[c]], d3[:, blocks[c]]])
             for c in range(PACK):
-                turn_and_add(lead_bank[:, c, :], [term[:, blocks[c]] for term in (at1[t], at2[t], at3, at4)])
+                turn_and_add(lead_bank[:, c, :], [term[:, blocks[c]] for term in (y1, minus_y2, d3, minus_d4)])
             first = ring.tile([P, PACK, P], F32, name="first")
             gain = ring.tile([P, PACK, P], F32, name="gain")
             nc.scalar.activation(out=first[:], in_=first_bank[:], func=COPY)
             nc.scalar.activation(out=gain[:], in_=lead_bank[:], func=RELU, scale=-1.0)
+            back = psum.tile([P, S], F32, name="acc")
             for c in range(PACK):
-                turn_and_add(larger_sum[c][:, t, :], [first[:, c, :], gain[:, c, :]])
+                turn_and_add(back[:, blocks[c]], [first[:, c, :], gain[:, c, :]])
+            nc.scalar.copy(out=z[:, t, :], in_=back[:])
 
+        c_offs = gather_words("c_offs", l_offs)
+        c_two = gather_words("c_two", l_two)
+        c_three = gather_words("c_three", l_three)
+        x_offs = (c_offs, gather_bytes("s_offs", l_offs, "s_offs"))
+        w1q_low = quantize("w1q0", deal("w1g0", raw1, "w1g0", 0, 2)[:].rearrange(flat))
+        y = {t: signed_pair(w1q_low, t, x_offs, t, (f"win{2 * t}", f"win{2 * t + 1}")) for t in range(2)}
+        x_two = (c_two, gather_bytes("s_two", l_two, "w1g0"))
+        w1q_high = quantize("w1q1", deal("w1g1", raw1, "w1g1", 2, 2)[:].rearrange(flat))
+        x_three = (c_three, gather_bytes("s_three", l_three, "w1g1"))
+
+        w2q_low = quantize("w2q0", deal("w2g0", raw2, "w2g0", 0, 2)[:].rearrange(flat))
+        at1 = {t: fetch(f"at1_{t}", y[t][0], l1) for t in range(2)}
+        at2 = {t: fetch(f"at2_{t}", y[t][1], l2) for t in range(2)}
+        w2q_high = quantize("w2q1", deal("w2g1", raw2, "w1q0_codes", 2, 2)[:].rearrange(flat))
+        d, at3, at4 = {}, {}, {}
+        for t in range(2):
+            d[t] = signed_pair(w2q_low, t, x_two, t, (f"win{4 + 2 * t}", f"win{5 + 2 * t}"))
+            at3[t] = fetch(f"at3_{t}", d[t][0], l3)
+            at4[t] = fetch(f"at4_{t}", d[t][1], l4)
+        y[2] = signed_pair(w1q_high, 0, x_offs, 2, ("win0", "win1"))
+        at1[2] = fetch("at1_2", y[2][0], l1)
+        at2[2] = fetch("at2_2", y[2][1], l2)
+        d[2] = signed_pair(w2q_high, 0, x_two, 2, ("win2", "win3"))
+        at3[2] = fetch("at3_2", d[2][0], l3)
+        at4[2] = fetch("at4_2", d[2][1], l4)
+        y_acc = product(w1q_high, 1, x_offs)
+        d_acc = product(w2q_high, 1, x_two)
+        w3q = quantize("w3q", deal("w3g", raw3, "w2q1_codes")[:].rearrange(flat))
+        y_last = emptied("y_last", y_acc, ga_abs[:, 3:4], 2 * S, "win4")
+        d_last = emptied("d_last", d_acc, ga_abs[:, 3:4], 2 * S, "win5")
+        at1[3] = fetch("at1_3", y_last, l1)
+        at2[3] = fetch("at2_3", y_last, l2)
+        first_sum = keep.tile([P, S], F32, name="first_sum")
+        second_sum = keep.tile([P, S], F32, name="second_sum")
+        nc.vector.tensor_tensor(first_sum[:], d_last[:].indirect(l3[:]), at1[3][:], ALU.add)
+        nc.vector.tensor_tensor(second_sum[:], d_last[:].indirect(l4[:]), at2[3][:], ALU.add)
+        for t in range(2):
+            larger_on_tensor(t, at1[t], at2[t], at3[t], at4[t])
+        b = [emptied(f"b{u}", product(w3q, u, x_three), 1.0, V if u == PACK - 1 else 2 * V) for u in range(PACK)]
+        larger_on_tensor(2, at1[2], at2[2], at3[2], at4[2])
         zg = keep.tile([P, PACK, P, PACK], BF16, name="zg", align_bytes=64)
-        for c in range(PACK):
-            m = slice(c * P // PACK, (c + 1) * P // PACK)
-            nc.scalar.copy(out=zg[:, :, m, :], in_=larger_sum[c][:].rearrange("p j (m t) -> p t m j", t=PACK))
 
         z2 = keep.tile([P, PACK, V], BF16, name="z2")
         z2g = keep.tile([P, V, PACK], BF16, name="z2g", align_bytes=64)
@@ -210,7 +217,7 @@ def tile_picked_twkpathbwindthree_none_p_kernel(
 
         def finish_z2(t, start, stop):
             nc.vector.scalar_tensor_tensor(
-                z2[:, t, start:stop], diffs[t, start][:], gb_signed[:, t : t + 1], b[t][:, start:stop], ALU.mult, ALU.mult
+                z2[:, t, start:stop], diffs[t, start], gb_signed[:, t : t + 1], b[t][:, start:stop], ALU.mult, ALU.mult
             )
 
         def weave_z2(start, stop, copy):
@@ -225,18 +232,23 @@ def tile_picked_twkpathbwindthree_none_p_kernel(
             nc.vector.tensor_copy(at6[:], b[t][:].indirect(l6[:]))
             if t > 0:
                 finish_z2(t - 1, 0, V)
-            diffs[t, 0] = ring.tile([P, V], F32, name="diff")
-            nc.vector.tensor_tensor(diffs[t, 0][:], b[t][:].indirect(l5[:]), at6[:], ALU.subtract)
-        zq = quantize("zq", zg[:].rearrange(flat))
-        at6 = keep.tile([P, V], F32, name="at6_last", tag="zg", align_bytes=64)
+            else:
+                nc.vector.tensor_tensor(z[:, last, :], first_sum[:], second_sum[:], ALU.max)
+                nc.scalar.copy(out=zg[:].rearrange("p t m j -> p m j t"), in_=z[:].rearrange("p j (m t) -> p m j t", t=PACK))
+            diff = ring.tile([P, V], F32, name="diff")
+            diffs[t, 0] = diff[:]
+            nc.vector.tensor_tensor(diff[:], b[t][:].indirect(l5[:]), at6[:], ALU.subtract)
+        at6 = ring.tile([P, V], F32, name="at6")
         for h in range(2):
             nc.vector.tensor_copy(at6[:, cols(h)], b[last][:].indirect(half_of(l6, h)))
         finish_z2(last - 1, 0, V)
+        zq = quantize("zq", zg[:].rearrange(flat))
+        diff_last = keep.tile([P, V], F32, name="diff_last", tag="zg", align_bytes=64)
         pieces = [(0, HALF), (HALF, HALF + P), (HALF + P, V)]
         for i, (start, stop) in enumerate(pieces):
-            diffs[last, start] = ring.tile([P, stop - start], F32, name="diff")
+            diffs[last, start] = diff_last[:, start:stop]
             entries = l5[:, start // STRIPE : stop // STRIPE]
-            nc.vector.tensor_tensor(diffs[last, start][:], b[last][:].indirect(entries), at6[:, start:stop], ALU.subtract)
+            nc.vector.tensor_tensor(diffs[last, start], b[last][:].indirect(entries), at6[:, start:stop], ALU.subtract)
             if i > 0:
                 finish_z2(last, *pieces[i - 1])
                 weave_z2(*pieces[i - 1], nc.scalar.copy)
@@ -258,17 +270,17 @@ def tile_picked_twkpathbwindthree_none_p_kernel(
 
         minus, plus = [], []
         for t in range(PACK):
-            minus.append(keep.tile([P, 2 * V], F32, name=f"minus{t}", tag=f"y{t}"))
+            minus.append(keep.tile([P, 2 * V], F32, name=f"minus{t}", tag=f"win{t}"))
             plus.append(keep.tile([P, V], F32, name=f"plus{t}"))
             cuts = pieces if t == 0 else [(0, V)]
-            accs = [product(zq, t, (z2_codes[:, start:stop], z2_scales[:, start:stop]), t > 0) for start, stop in cuts]
+            accs = [product(zq, t, (z2_codes[:, start:stop], z2_scales[:, start:stop])) for start, stop in cuts]
             for acc, (start, stop) in zip(accs, cuts):
                 nc.scalar.activation(out=minus[t][:, start:stop], in_=acc[:], func=COPY, scale=-0.0625)
                 if start == 0:
                     nc.scalar.activation(out=plus[t][:, start:stop], in_=acc[:], func=COPY, scale=0.0625)
             for acc, (start, stop) in list(zip(accs, cuts))[1:]:
                 nc.scalar.activation(out=plus[t][:, start:stop], in_=acc[:], func=COPY, scale=0.0625)
-        st = [keep.tile([P, 2 * V], F32, name=f"st{t}", tag=f"d{t}") for t in range(PACK)]
+        st = [keep.tile([P, 2 * V], F32, name=f"st{t}", tag=f"win{PACK + t}") for t in range(PACK)]
         at8 = [keep.tile([P, V], F32, name=f"at8_{t}") for t in range(PACK)]
         su = [keep.tile([P, V], F32, name=f"su{t}") for t in range(PACK)]
         su_half = [keep.tile([P, 2 * V], F32, name=f"su_half{t}", tag=f"b{t}") for t in range(PACK)]

from contextlib import ExitStack

import concourse.mybir as mybir
from concourse.masks import make_identity

K, T, S, V, H = 512, 2048, 512, 512, 512
FLOPS = 2 * K * H * (S + S + V) + 2 * H * S * V

F32 = mybir.dt.float32
BF16 = mybir.dt.bfloat16
I32 = mybir.dt.int32
U32 = mybir.dt.uint32
U16 = mybir.dt.uint16
U8 = mybir.dt.uint8
FP8X4 = mybir.dt.float8_e4m3fn_x4
ALU = mybir.AluOpType
COPY = mybir.ActivationFunctionType.Copy
RELU = mybir.ActivationFunctionType.Relu

P = 128
PACK = 4
HALF = 256
STRIPE = 16


def tile_picked_twkpathbwindthree_none_p_kernel(
    tc, x_words, x_scales, w1, w2, w3, ga, gb, offs, two, n1, n2, n3, n4, three, n5, n6, n7, n8, n9, out
):
    nc = tc.nc
    with ExitStack() as ctx:
        lists = ctx.enter_context(tc.tile_pool(name="lists", bufs=1))
        keep = ctx.enter_context(tc.tile_pool(name="keep", bufs=1))
        ring = ctx.enter_context(tc.tile_pool(name="ring", bufs=2))
        psum = ctx.enter_context(tc.psum_pool(name="psum", bufs=8))

        def load_list(name, src):
            tile = lists.tile([P, S // STRIPE], U16, name=name)
            nc.sync.dma_start(tile[:], src)
            return tile

        def load_weight(name, src):
            raw = keep.tile([P, PACK, H], F32, name=name)
            nc.sync.dma_start(out=raw[:], in_=src.rearrange("(p j) c -> p j c", j=PACK))
            return raw

        def half_of(offsets, h):
            return offsets[:, h * HALF // STRIPE : (h + 1) * HALF // STRIPE]

        def cols(h):
            return slice(h * HALF, (h + 1) * HALF)

        plane = keep.tile([P, T], U8, name="plane", align_bytes=64)
        nc.vector.memset(plane[:].bitcast(I32), 0)
        l_offs = load_list("l_offs", offs)
        for q in range(4):
            nc.scalar.dma_start(out=plane[32 * q : 32 * q + 4, :].bitcast(I32), in_=x_scales[0, 4 * q : 4 * q + 4, :].bitcast(I32))
        words = keep.tile([P, T], U32, name="words", align_bytes=64)
        nc.sync.dma_start(out=words[:].bitcast(I32), in_=x_words[0].rearrange("p n t -> p (n t)").bitcast(I32))
        l_two = load_list("l_two", two)
        l_three = load_list("l_three", three)
        raw1 = load_weight("raw1", w1)
        raw2 = load_weight("raw2", w2)
        l1 = load_list("l1", n1)
        l3 = load_list("l3", n3)
        raw3 = load_weight("raw3", w3)
        l2 = load_list("l2", n2)
        l4 = load_list("l4", n4)
        l6 = load_list("l6", n6)
        l5 = load_list("l5", n5)
        l7 = load_list("l7", n7)
        l8 = load_list("l8", n8)
        l9 = load_list("l9", n9)

        ga_t = keep.tile([P, PACK], F32, name="ga_t")
        gb_t = keep.tile([P, PACK], F32, name="gb_t")
        nc.gpsimd.dma_start(out=ga_t[:], in_=ga.rearrange("(p t) o -> p (t o)", t=PACK))
        nc.gpsimd.dma_start(out=gb_t[:], in_=gb.rearrange("(p t) o -> p (t o)", t=PACK))
        twice = keep.tile([P, PACK], F32, name="twice")
        sign = keep.tile([P, PACK], F32, name="sign")
        ga_abs = keep.tile([P, PACK], F32, name="ga_abs")
        gb_signed = keep.tile([P, PACK], F32, name="gb_signed")
        nc.gpsimd.tensor_scalar(twice[:], ga_t[:], 0.0, 2.0, ALU.is_ge, ALU.mult)
        nc.gpsimd.tensor_scalar(sign[:], twice[:], 1.0, -1.0, ALU.mult, ALU.add)
        nc.gpsimd.tensor_tensor(ga_abs[:], ga_t[:], sign[:], ALU.mult)
        ga_minus = keep.tile([P, PACK], F32, name="ga_minus")
        nc.gpsimd.tensor_scalar(ga_minus[:], ga_abs[:], -1.0, 0.0, ALU.mult, ALU.add)
        nc.gpsimd.tensor_tensor(gb_signed[:], gb_t[:], sign[:], ALU.mult)

        def gather_bytes(name, offsets, tag):
            picked = keep.tile([P, S], U8, name=name, tag=tag, align_bytes=64)
            nc.vector.tensor_copy(picked[:], plane[:].indirect(offsets[:]))
            return picked[:]

        def gather_words(name, offsets):
            picked = keep.tile([P, S], U32, name=name, align_bytes=64)
            nc.vector.tensor_copy(picked[:], words[:].indirect(offsets[:]))
            return picked[:]

        def deal(name, raw, tag, first=0, count=PACK):
            grouped = keep.tile([P, count, P, PACK], BF16, name=name, tag=tag, align_bytes=64)
            nc.scalar.copy(
                out=grouped[:].rearrange("p t m j -> p m j t"),
                in_=raw[:].rearrange("p j (m t) -> p m j t", t=PACK)[:, :, :, first : first + count],
            )
            return grouped

        def quantize(name, grouped_flat):
            width = grouped_flat.shape[1] // PACK
            codes = keep.tile([P, width], U32, name=name + "_codes", align_bytes=64)
            scales = keep.tile([P, width], U8, name=name + "_scales", align_bytes=64)
            nc.vector.quantize_mx(out=codes[:].bitcast(FP8X4), scales=scales[:], in_=grouped_flat)
            return codes, scales

        def product(stationary, t, moving):
            acc = psum.tile([P, moving[1].shape[1]], F32, name="acc")
            rows = slice(t * P, (t + 1) * P)
            nc.tensor.matmul_mx(
                out=acc[:],
                lhsT=stationary[0][:, rows].bitcast(FP8X4),
                lhsT_scale=stationary[1][:, rows],
                rhs=moving[0].bitcast(FP8X4),
                rhs_scale=moving[1],
                start=True,
                stop=True,
            )
            return acc

        def emptied(name, acc, scale, width=S, tag=None):
            tile = keep.tile([P, width], F32, name=name, tag=tag or name)
            nc.scalar.activation(out=tile[:, :S], in_=acc[:], func=COPY, scale=scale)
            return tile

        flat = "p t m j -> p (t m j)"
        ident = keep.tile([P, P], F32, name="ident")
        make_identity(nc, ident[:])

        def signed_pair(wq, u, moving, t, tags):
            acc = product(wq, u, moving)
            return (
                emptied("plain", acc, ga_abs[:, t : t + 1], 2 * S, tags[0]),
                emptied("negated", acc, ga_minus[:, t : t + 1], 2 * S, tags[1]),
            )

        def turn_and_add(bank, terms):
            for i, term in enumerate(terms):
                nc.tensor.matmul(bank, term, ident[:], start=i == 0, stop=i == len(terms) - 1, is_transpose=True)

        def fetch(name, window, offsets, tag=None):
            tile = keep.tile([P, S], F32, name=name, tag=tag or name, align_bytes=64)
            nc.vector.tensor_copy(tile[:], window[:].indirect(offsets[:]))
            return tile

        z = keep.tile([P, PACK, S], BF16, name="z")

        def larger_on_tensor(t, y1, minus_y2, d3, minus_d4):
            first_bank = psum.tile([P, PACK, P], F32, name="acc")
            lead_bank = psum.tile([P, PACK, P], F32, name="acc")
            blocks = [slice(c * P, (c + 1) * P) for c in range(PACK)]
            for c in range(PACK):
                turn_and_add(first_bank[:, c, :], [y1[:, blocks[c]], d3[:, blocks[c]]])
            for c in range(PACK):
                turn_and_add(lead_bank[:, c, :], [term[:, blocks[c]] for term in (y1, minus_y2, d3, minus_d4)])
            first = ring.tile([P, PACK, P], F32, name="first")
            gain = ring.tile([P, PACK, P], F32, name="gain")
            nc.scalar.activation(out=first[:], in_=first_bank[:], func=COPY)
            nc.scalar.activation(out=gain[:], in_=lead_bank[:], func=RELU, scale=-1.0)
            back = psum.tile([P, S], F32, name="acc")
            for c in range(PACK):
                turn_and_add(back[:, blocks[c]], [first[:, c, :], gain[:, c, :]])
            nc.scalar.copy(out=z[:, t, :], in_=back[:])

        c_offs = gather_words("c_offs", l_offs)
        c_two = gather_words("c_two", l_two)
        c_three = gather_words("c_three", l_three)
        x_offs = (c_offs, gather_bytes("s_offs", l_offs, "s_offs"))
        w1q_low = quantize("w1q0", deal("w1g0", raw1, "w1g0", 0, 2)[:].rearrange(flat))
        y = {t: signed_pair(w1q_low, t, x_offs, t, (f"win{2 * t}", f"win{2 * t + 1}")) for t in range(2)}
        x_two = (c_two, gather_bytes("s_two", l_two, "w1g0"))
        w1q_high = quantize("w1q1", deal("w1g1", raw1, "w1g1", 2, 2)[:].rearrange(flat))
        x_three = (c_three, gather_bytes("s_three", l_three, "w1g1"))

        w2q_low = quantize("w2q0", deal("w2g0", raw2, "w2g0", 0, 2)[:].rearrange(flat))
        at1 = {t: fetch(f"at1_{t}", y[t][0], l1) for t in range(2)}
        at2 = {t: fetch(f"at2_{t}", y[t][1], l2) for t in range(2)}
        w2q_high = quantize("w2q1", deal("w2g1", raw2, "w1q0_codes", 2, 2)[:].rearrange(flat))
        d, at3, at4 = {}, {}, {}
        for t in range(2):
            d[t] = signed_pair(w2q_low, t, x_two, t, (f"win{4 + 2 * t}", f"win{5 + 2 * t}"))
            at3[t] = fetch(f"at3_{t}", d[t][0], l3)
            at4[t] = fetch(f"at4_{t}", d[t][1], l4)
        y[2] = signed_pair(w1q_high, 0, x_offs, 2, ("win0", "win1"))
        at1[2] = fetch("at1_2", y[2][0], l1)
        at2[2] = fetch("at2_2", y[2][1], l2)
        d[2] = signed_pair(w2q_high, 0, x_two, 2, ("win2", "win3"))
        at3[2] = fetch("at3_2", d[2][0], l3)
        at4[2] = fetch("at4_2", d[2][1], l4)
        y_acc = product(w1q_high, 1, x_offs)
        d_acc = product(w2q_high, 1, x_two)
        w3q = quantize("w3q", deal("w3g", raw3, "w2q1_codes")[:].rearrange(flat))
        y_last = emptied("y_last", y_acc, ga_abs[:, 3:4], 2 * S, "win4")
        d_last = emptied("d_last", d_acc, ga_abs[:, 3:4], 2 * S, "win5")
        at1[3] = fetch("at1_3", y_last, l1)
        at2[3] = fetch("at2_3", y_last, l2)
        first_sum = keep.tile([P, S], F32, name="first_sum")
        second_sum = keep.tile([P, S], F32, name="second_sum")
        nc.vector.tensor_tensor(first_sum[:], d_last[:].indirect(l3[:]), at1[3][:], ALU.add)
        nc.vector.tensor_tensor(second_sum[:], d_last[:].indirect(l4[:]), at2[3][:], ALU.add)
        for t in range(2):
            larger_on_tensor(t, at1[t], at2[t], at3[t], at4[t])
        b = [emptied(f"b{u}", product(w3q, u, x_three), 1.0, V if u == PACK - 1 else 2 * V) for u in range(PACK)]
        larger_on_tensor(2, at1[2], at2[2], at3[2], at4[2])
        zg = keep.tile([P, PACK, P, PACK], BF16, name="zg", align_bytes=64)

        z2 = keep.tile([P, PACK, V], BF16, name="z2")
        z2g = keep.tile([P, V, PACK], BF16, name="z2g", align_bytes=64)
        diffs = {}

        def finish_z2(t, start, stop):
            nc.vector.scalar_tensor_tensor(
                z2[:, t, start:stop], diffs[t, start], gb_signed[:, t : t + 1], b[t][:, start:stop], ALU.mult, ALU.mult
            )

        def weave_z2(start, stop, copy):
            copy(
                out=z2g[:, start:stop, :].rearrange("p (c i) j -> p c j i", i=PACK),
                in_=z2[:, :, start:stop].rearrange("p j (c i) -> p c j i", i=PACK),
            )

        last = PACK - 1
        for t in range(last):
            at6 = ring.tile([P, V], F32, name="at6")
            nc.vector.tensor_copy(at6[:], b[t][:].indirect(l6[:]))
            if t > 0:
                finish_z2(t - 1, 0, V)
            else:
                nc.vector.tensor_tensor(z[:, last, :], first_sum[:], second_sum[:], ALU.max)
                nc.scalar.copy(out=zg[:].rearrange("p t m j -> p m j t"), in_=z[:].rearrange("p j (m t) -> p m j t", t=PACK))
            diff = ring.tile([P, V], F32, name="diff")
            diffs[t, 0] = diff[:]
            nc.vector.tensor_tensor(diff[:], b[t][:].indirect(l5[:]), at6[:], ALU.subtract)
        at6 = ring.tile([P, V], F32, name="at6")
        for h in range(2):
            nc.vector.tensor_copy(at6[:, cols(h)], b[last][:].indirect(half_of(l6, h)))
        finish_z2(last - 1, 0, V)
        zq = quantize("zq", zg[:].rearrange(flat))
        diff_last = keep.tile([P, V], F32, name="diff_last", tag="zg", align_bytes=64)
        pieces = [(0, HALF), (HALF, HALF + P), (HALF + P, V)]
        for i, (start, stop) in enumerate(pieces):
            diffs[last, start] = diff_last[:, start:stop]
            entries = l5[:, start // STRIPE : stop // STRIPE]
            nc.vector.tensor_tensor(diffs[last, start], b[last][:].indirect(entries), at6[:, start:stop], ALU.subtract)
            if i > 0:
                finish_z2(last, *pieces[i - 1])
                weave_z2(*pieces[i - 1], nc.scalar.copy)
        finish_z2(last, *pieces[-1])
        z2_codes = keep.tile([P, V], U32, name="z2_codes", align_bytes=64)
        z2_scales = keep.tile([P, V], U8, name="z2_scales", align_bytes=64)

        def quantize_z2(start, stop):
            nc.vector.quantize_mx(
                out=z2_codes[:, start:stop].bitcast(FP8X4),
                scales=z2_scales[:, start:stop],
                in_=z2g[:, start:stop, :].rearrange("p v j -> p (v j)"),
            )

        quantize_z2(*pieces[0])
        weave_z2(*pieces[-1], nc.vector.tensor_copy)
        for piece in pieces[1:]:
            quantize_z2(*piece)

        minus, plus = [], []
        for t in range(PACK):
            minus.append(keep.tile([P, 2 * V], F32, name=f"minus{t}", tag=f"win{t}"))
            plus.append(keep.tile([P, V], F32, name=f"plus{t}"))
            cuts = pieces if t == 0 else [(0, V)]
            accs = [product(zq, t, (z2_codes[:, start:stop], z2_scales[:, start:stop])) for start, stop in cuts]
            for acc, (start, stop) in zip(accs, cuts):
                nc.scalar.activation(out=minus[t][:, start:stop], in_=acc[:], func=COPY, scale=-0.0625)
                if start == 0:
                    nc.scalar.activation(out=plus[t][:, start:stop], in_=acc[:], func=COPY, scale=0.0625)
            for acc, (start, stop) in list(zip(accs, cuts))[1:]:
                nc.scalar.activation(out=plus[t][:, start:stop], in_=acc[:], func=COPY, scale=0.0625)
        st = [keep.tile([P, 2 * V], F32, name=f"st{t}", tag=f"win{PACK + t}") for t in range(PACK)]
        at8 = [keep.tile([P, V], F32, name=f"at8_{t}") for t in range(PACK)]
        su = [keep.tile([P, V], F32, name=f"su{t}") for t in range(PACK)]
        su_half = [keep.tile([P, 2 * V], F32, name=f"su_half{t}", tag=f"b{t}") for t in range(PACK)]
        result = [keep.tile([P, V], F32, name=f"result{t}") for t in range(PACK)]
        out_rows = out.rearrange("(p t) v -> p t v", t=PACK)

        def stage7(t):
            if t > 0:
                nc.vector.tensor_tensor(st[t][:, :V], minus[t][:].indirect(l7[:]), plus[t][:], ALU.add)
                return
            for h in range(2):
                nc.vector.tensor_tensor(st[t][:, cols(h)], minus[t][:].indirect(half_of(l7, h)), plus[t][:, cols(h)], ALU.add)

        def stage8(t):
            nc.vector.tensor_copy(at8[t][:], st[t][:].indirect(l8[:]))

        def larger(t):
            nc.vector.tensor_tensor(su[t][:], st[t][:, :V], at8[t][:], ALU.max)
            nc.scalar.activation(out=su_half[t][:, :V], in_=su[t][:], func=COPY, scale=0.5)

        def stage9(t):
            if t < PACK - 1:
                nc.vector.tensor_tensor(result[t][:], su_half[t][:].indirect(l9[:]), su[t][:], ALU.add)
                nc.sync.dma_start(out=out_rows[:, t, :], in_=result[t][:])
                return
            for h in range(2):
                nc.vector.tensor_tensor(result[t][:, cols(h)], su_half[t][:].indirect(half_of(l9, h)), su[t][:, cols(h)], ALU.add)
                nc.sync.dma_start(out=out_rows[:, t, cols(h)], in_=result[t][:, cols(h)])

        stages = [stage7, stage8, larger, stage9]
        for wave in range(PACK + len(stages) - 1):
            for i, stage in enumerate(stages):
                if 0 <= wave - i < PACK:
                    stage(wave - i)
